import numpy as np
import ml_dtypes


def mxq(x, axis, fmt="e4m3"):
    dtype, down = {"e4m3": (ml_dtypes.float8_e4m3fn, 7), "e5m2": (ml_dtypes.float8_e5m2, 14)}[fmt]
    v = np.moveaxis(np.asarray(x, np.float32).astype(ml_dtypes.bfloat16).astype(np.float64), axis, -1)
    blocks = v.reshape(v.shape[:-1] + (-1, 32))
    amax = np.abs(blocks).max(-1, keepdims=True)
    byte = np.maximum(np.where(amax > 0, np.frexp(amax)[1] - 1 + 127, 0) - down, 1)
    scale = np.exp2(byte - 127.0)
    codes = (blocks / scale).astype(np.float32).astype(dtype).astype(np.float64)
    return np.moveaxis((codes * scale).reshape(v.shape), -1, axis)


WIDE = False


def mx_kscale(k):
    if not WIDE:
        return np.ones(k)
    levels = np.array([10, -10, 5, -5, 0])
    if k % 512:
        return np.exp2(np.random.permutation(np.resize(levels, k // 32))).repeat(32)
    a = np.empty((k // 512, 16))
    for p in range(k // 512):
        a[p, :8] = np.random.permutation(np.resize(levels, 8))
        for g in range(8):
            far = levels[np.abs(levels - a[p, g]) >= 10]
            a[p, g + 8] = far[np.random.randint(len(far))]
    return np.exp2(a.ravel()).repeat(32)


def f64(x):
    return np.asarray(x).astype(np.float64)


def striped(idx):
    return np.tile(idx.reshape(-1, 16).T, (8, 1)).astype(np.uint16)


def unstriped(offs):
    return offs[:16].T.reshape(-1).astype(np.int64)


def silu(v):
    return v / (1.0 + np.exp(-np.maximum(v, -700.0)))


K, T, D, S, V, H, N = 1024, 2048, 2, 768, 384, 512, 128


def setup_inputs():
    n = np.random.standard_normal
    s = mx_kscale(K)[:, None]
    u = mx_kscale(H)
    return {
        "xT": (n((K, T)) * s).astype(np.float32),
        "w1": (n((K, H)) / np.sqrt(K) / s * u).astype(np.float32),
        "w2": (n((H, N)) / np.sqrt(H) / u[:, None]).astype(np.float32),
        "gate": np.tile(np.random.uniform(0.2, 1.0, (D, 1, V)) / np.sqrt(D), (1, N, 1)).astype(np.float32),
        "offs": striped(np.random.permutation(T)[:S]),
        "pos1": striped(np.random.permutation(S)[:V]),
        "pos2": striped(np.random.permutation(S)[:V]),
    }


def reference(xT, w1, w2, gate, offs, pos1, pos2):
    idx = unstriped(offs)
    xq = mxq(f64(xT)[:, idx], 0, "e4m3")
    h = silu(mxq(f64(w1), 0, "e4m3").T @ xq)
    y = mxq(f64(w2), 0, "e4m3").T @ mxq(h, 0, "e4m3")
    return sum(f64(gate[d]) * y[:, unstriped(p)] for d, p in enumerate((pos1, pos2)))

@@ -1,0 +1,211 @@
+from contextlib import ExitStack
+
+import concourse.mybir as mybir
+
+K, T, S, V, H, N = 1024, 2048, 768, 384, 512, 128
+FLOPS = 2 * S * H * K + 2 * S * N * H
+
+F32 = mybir.dt.float32
+BF16 = mybir.dt.bfloat16
+U32 = mybir.dt.uint32
+U8 = mybir.dt.uint8
+U16 = mybir.dt.uint16
+FP8X4 = mybir.dt.float8_e4m3fn_x4
+MULT = mybir.AluOpType.mult
+ADD = mybir.AluOpType.add
+SILU = mybir.ActivationFunctionType.Silu
+
+P = 128
+PACK = 4
+PICK = 256
+CHUNK = 128
+CHUNKS = S // CHUNK
+
+
+def tile_picked_sub_mlp_silu_sub_e_kernel(tc, xT, w1, w2, gate, offs, pos1, pos2, out):
+    nc = tc.nc
+    with ExitStack() as ctx:
+        lists = ctx.enter_context(tc.tile_pool(name="lists", bufs=1))
+        held = ctx.enter_context(tc.tile_pool(name="held", bufs=1))
+        psum = ctx.enter_context(tc.psum_pool(name="psum", bufs=1))
+
+        offs_sb = lists.tile([P, S // 16], U16, name="offs_sb")
+        pos1_sb = lists.tile([P, V // 16], U16, name="pos1_sb")
+        pos2_sb = lists.tile([P, V // 16], U16, name="pos2_sb")
+
+        x_rows = xT.rearrange("(s p j) t -> s j p t", s=2, j=PACK)
+        w1_rows = w1.rearrange("(s p j) h -> s p j h", s=2, j=PACK)
+
+        x_plane = [[held.tile([P, T], F32, name="x_plane_%d_%d" % (s, j)) for j in range(PACK)] for s in range(2)]
+        w1_raw = [held.tile([P, PACK, H], F32, name="w1_raw_%d" % s) for s in range(2)]
+        w1_grouped = [held.tile([P, PACK, P, PACK], BF16, name="w1_grouped_%d" % s, align_bytes=64) for s in range(2)]
+        w1_codes = [held.tile([P, H], U32, name="w1_codes_%d" % s, align_bytes=64) for s in range(2)]
+        w1_scales = [held.tile([P, H], U8, name="w1_scales_%d" % s, align_bytes=64) for s in range(2)]
+        w2_raw = held.tile([P, PACK, N], F32, name="w2_raw")
+        w2_grouped = held.tile([P, N, PACK], BF16, name="w2_grouped", align_bytes=64)
+        w2_codes = held.tile([P, N], U32, name="w2_codes", align_bytes=64)
+        w2_scales = held.tile([P, N], U8, name="w2_scales", align_bytes=64)
+        gate_sb = held.tile([P, 2, V], F32, name="gate_sb")
+
+        picked = [held.tile([P, PACK, S], F32, name="picked_0"), held.tile([P, 2, S], F32, name="picked_1")]
+        x_grouped = [held.tile([P, S, PACK], BF16, name="x_grouped_%d" % s, align_bytes=64) for s in range(2)]
+        x_codes = [held.tile([P, S], U32, name="x_codes_%d" % s, align_bytes=64) for s in range(2)]
+        x_scales = [held.tile([P, S], U8, name="x_scales_%d" % s, align_bytes=64) for s in range(2)]
+
+        h_grouped = [held.tile([P, CHUNK, PACK], BF16, name="h_grouped_%d" % c, align_bytes=64) for c in range(CHUNKS)]
+        h_codes = [held.tile([P, CHUNK], U32, name="h_codes_%d" % c, align_bytes=64) for c in range(CHUNKS)]
+        h_scales = [held.tile([P, CHUNK], U8, name="h_scales_%d" % c, align_bytes=64) for c in range(CHUNKS)]
+        y_sb = held.tile([P, S], F32, name="y_sb")
+
+        h_bank = [psum.tile([P, PACK, CHUNK], F32, name="h_bank_%d" % c) for c in range(CHUNKS)]
+        y_bank = [psum.tile([P, CHUNK], F32, name="y_bank_%d" % b) for b in range(2)]
+
+        warm = held.tile([P, 1], F32, name="warm")
+        warm_out = held.tile([P, 1], F32, name="warm_out")
+        nc.vector.memset(warm[:], 0.0)
+        nc.scalar.activation(warm_out[:], warm[:], SILU)
+
+        nc.sync.dma_start(offs_sb[:], offs)
+        nc.sync.dma_start(x_plane[0][0][:], x_rows[0, 0])
+        nc.sync.dma_start(w1_raw[0][:], w1_rows[0])
+        for j in range(1, PACK):
+            nc.sync.dma_start(x_plane[0][j][:], x_rows[0, j])
+        nc.sync.dma_start(w1_raw[1][:, 0:2, :], w1_rows[1, :, 0:2, :])
+        for j in range(3):
+            nc.sync.dma_start(x_plane[1][j][:], x_rows[1, j])
+        nc.sync.dma_start(w1_raw[1][:, 2:4, :], w1_rows[1, :, 2:4, :])
+        nc.sync.dma_start(x_plane[1][3][:], x_rows[1, 3])
+        nc.sync.dma_start(w2_raw[:], w2.rearrange("(p j) n -> p j n", j=PACK))
+        nc.sync.dma_start(pos1_sb[:], pos1)
+        nc.sync.dma_start(pos2_sb[:], pos2)
+        nc.sync.dma_start(gate_sb[:], gate.rearrange("d n v -> n d v"))
+
+        def pick_plain(s, j):
+            nc.vector.tensor_copy(picked[s][:, j, :], x_plane[s][j][:].indirect(offs_sb[:]))
+
+        def pick_stepped(j, c):
+            cols = slice(c * PICK, (c + 1) * PICK)
+            nc.vector.tensor_copy(
+                x_grouped[1][:, cols, j],
+                x_plane[1][j][:].indirect(offs_sb[:, c * PICK // 16 : (c + 1) * PICK // 16]),
+            )
+
+        def group_w1(s, a, b):
+            nc.scalar.copy(
+                w1_grouped[s][:, :, :, a:b].rearrange("p t m j -> p m t j"),
+                w1_raw[s][:, a:b, :].rearrange("p j (m t) -> p m t j", t=PACK),
+            )
+
+        def quantize_w1(s):
+            nc.vector.quantize_mx(
+                out=w1_codes[s][:].bitcast(FP8X4), scales=w1_scales[s][:], in_=w1_grouped[s][:].rearrange("p t m j -> p (t m j)")
+            )
+
+        def quantize_x(s, a, b):
+            nc.vector.quantize_mx(
+                out=x_codes[s][:, a:b].bitcast(FP8X4),
+                scales=x_scales[s][:, a:b],
+                in_=x_grouped[s][:, a:b, :].rearrange("p n j -> p (n j)"),
+            )
+
+        def hidden_pass(c, t, s):
+            cols = slice(c * CHUNK, (c + 1) * CHUNK)
+            nc.tensor.matmul_mx(
+                out=h_bank[c][:, t, :],
+                lhsT=w1_codes[s][:, t * P : (t + 1) * P].bitcast(FP8X4),
+                lhsT_scale=w1_scales[s][:, t * P : (t + 1) * P],
+                rhs=x_codes[s][:, cols].bitcast(FP8X4),
+                rhs_scale=x_scales[s][:, cols],
+                start=(s == 0),
+                stop=(s == 1),
+            )
+
+        group_w1(0, 0, 4)
+        pick_plain(0, 0)
+        pick_plain(0, 1)
+        quantize_w1(0)
+        pick_plain(0, 2)
+        pick_plain(0, 3)
+        nc.scalar.copy(
+            x_grouped[0][:].rearrange("p (c i) j -> p c j i", i=4),
+            picked[0][:].rearrange("p j (c i) -> p c j i", i=4),
+        )
+        group_w1(1, 0, 2)
+        pick_plain(1, 0)
+        pick_plain(1, 1)
+        quantize_x(0, 0, 512)
+        quantize_x(0, 512, 768)
+        nc.scalar.copy(x_grouped[1][:, :, 0:2], picked[1][:].rearrange("p j n -> p n j"))
+        for c in range(3):
+            pick_stepped(2, c)
+        group_w1(1, 2, 4)
+        quantize_w1(1)
+        for c in range(CHUNKS):
+            hidden_pass(c, 0, 0)
+
+        pick_stepped(3, 0)
+        pick_stepped(3, 1)
+        quantize_x(1, 0, 256)
+        pick_stepped(3, 2)
+        quantize_x(1, 256, 512)
+        quantize_x(1, 512, 768)
+        nc.scalar.copy(w2_grouped[:], w2_raw[:].rearrange("p j n -> p n j"))
+        nc.vector.quantize_mx(
+            out=w2_codes[:].bitcast(FP8X4), scales=w2_scales[:], in_=w2_grouped[:].rearrange("p n j -> p (n j)")
+        )
+
+        def hidden(c):
+            hidden_pass(c, 0, 1)
+            for t in range(1, PACK):
+                hidden_pass(c, t, 0)
+                hidden_pass(c, t, 1)
+            nc.scalar.activation(h_grouped[c][:], h_bank[c][:].rearrange("p t n -> p n t"), SILU)
+
+        def quantize_h(c):
+            nc.vector.quantize_mx(
+                out=h_codes[c][:].bitcast(FP8X4), scales=h_scales[c][:], in_=h_grouped[c][:].rearrange("p n t -> p (n t)")
+            )
+
+        def output(c):
+            nc.tensor.matmul_mx(
+                out=y_bank[c % 2][:],
+                lhsT=w2_codes[:].bitcast(FP8X4),
+                lhsT_scale=w2_scales[:],
+                rhs=h_codes[c][:].bitcast(FP8X4),
+                rhs_scale=h_scales[c][:],
+                start=True,
+                stop=True,
+            )
+            nc.vector.tensor_copy(y_sb[:, c * CHUNK : (c + 1) * CHUNK], y_bank[c % 2][:])
+
+        for step in range(CHUNKS + 2):
+            if step < CHUNKS:
+                hidden(step)
+            if 1 <= step <= CHUNKS:
+                quantize_h(step - 1)
+            if step >= 2:
+                output(step - 2)
+
+        half = V // 2
+        terms = [[held.tile([P, half], F32, name="term_%d_%d" % (a, d)) for d in range(2)] for a in range(2)]
+        sums = [held.tile([P, half], F32, name="sum_%d" % a) for a in range(2)]
+
+        def term(a, d):
+            pos = (pos1_sb, pos2_sb)[d]
+            nc.vector.tensor_tensor(
+                terms[a][d][:],
+                y_sb[:].indirect(pos[:, a * half // 16 : (a + 1) * half // 16]),
+                gate_sb[:, d, a * half : (a + 1) * half],
+                MULT,
+            )
+
+        def total(a):
+            nc.vector.tensor_tensor(sums[a][:], terms[a][0][:], terms[a][1][:], ADD)
+            nc.sync.dma_start(out[:, a * half : (a + 1) * half], sums[a][:])
+
+        term(0, 0)
+        term(0, 1)
+        term(1, 0)
+        total(0)
+        term(1, 1)
+        total(1)

@@ -19,7 +19,7 @@ P = 128
 PACK = 4
 PICK = 256
 CHUNK = 128
-CHUNKS = S // CHUNK
+ORDER = (0, 1, 4, 5, 2, 3)
 
 
 def tile_picked_sub_mlp_silu_sub_e_kernel(tc, xT, w1, w2, gate, offs, pos1, pos2, out):
@@ -36,28 +36,32 @@ def tile_picked_sub_mlp_silu_sub_e_kernel(tc, xT, w1, w2, gate, offs, pos1, pos2
         x_rows = xT.rearrange("(s p j) t -> s j p t", s=2, j=PACK)
         w1_rows = w1.rearrange("(s p j) h -> s p j h", s=2, j=PACK)
 
-        x_plane = [[held.tile([P, T], F32, name="x_plane_%d_%d" % (s, j)) for j in range(PACK)] for s in range(2)]
+        x_plane = [
+            [held.tile([P, T], F32, name="x_plane_%d_%d" % (s, j), tag="x_plane_%d_%d" % (s, j), align_bytes=64) for j in range(PACK)]
+            for s in range(2)
+        ]
         w1_raw = [held.tile([P, PACK, H], F32, name="w1_raw_%d" % s) for s in range(2)]
         w1_grouped = [held.tile([P, PACK, P, PACK], BF16, name="w1_grouped_%d" % s, align_bytes=64) for s in range(2)]
-        w1_codes = [held.tile([P, H], U32, name="w1_codes_%d" % s, align_bytes=64) for s in range(2)]
-        w1_scales = [held.tile([P, H], U8, name="w1_scales_%d" % s, align_bytes=64) for s in range(2)]
+        w1_scales = [held.tile([P, PACK, P], U8, name="w1_scales_%d" % s, align_bytes=64) for s in range(2)]
+        w1_codes = {}
         w2_raw = held.tile([P, PACK, N], F32, name="w2_raw")
         w2_grouped = held.tile([P, N, PACK], BF16, name="w2_grouped", align_bytes=64)
         w2_codes = held.tile([P, N], U32, name="w2_codes", align_bytes=64)
         w2_scales = held.tile([P, N], U8, name="w2_scales", align_bytes=64)
         gate_sb = held.tile([P, 2, V], F32, name="gate_sb")
 
-        picked = [held.tile([P, PACK, S], F32, name="picked_0"), held.tile([P, 2, S], F32, name="picked_1")]
+        picked_pair = held.tile([P, 2, 512], F32, name="picked_pair")
+        picked_all = held.tile([P, PACK, PICK], F32, name="picked_all")
         x_grouped = [held.tile([P, S, PACK], BF16, name="x_grouped_%d" % s, align_bytes=64) for s in range(2)]
         x_codes = [held.tile([P, S], U32, name="x_codes_%d" % s, align_bytes=64) for s in range(2)]
         x_scales = [held.tile([P, S], U8, name="x_scales_%d" % s, align_bytes=64) for s in range(2)]
 
-        h_grouped = [held.tile([P, CHUNK, PACK], BF16, name="h_grouped_%d" % c, align_bytes=64) for c in range(CHUNKS)]
-        h_codes = [held.tile([P, CHUNK], U32, name="h_codes_%d" % c, align_bytes=64) for c in range(CHUNKS)]
-        h_scales = [held.tile([P, CHUNK], U8, name="h_scales_%d" % c, align_bytes=64) for c in range(CHUNKS)]
+        h_grouped = [held.tile([P, CHUNK, PACK], BF16, name="h_grouped_%d" % c, align_bytes=64) for c in range(6)]
+        h_codes = [held.tile([P, CHUNK], U32, name="h_codes_%d" % c, align_bytes=64) for c in range(6)]
+        h_scales = [held.tile([P, CHUNK], U8, name="h_scales_%d" % c, align_bytes=64) for c in range(6)]
         y_sb = held.tile([P, S], F32, name="y_sb")
 
-        h_bank = [psum.tile([P, PACK, CHUNK], F32, name="h_bank_%d" % c) for c in range(CHUNKS)]
+        h_bank = [psum.tile([P, PACK, CHUNK], F32, name="h_bank_%d" % c) for c in range(6)]
         y_bank = [psum.tile([P, CHUNK], F32, name="y_bank_%d" % b) for b in range(2)]
 
         warm = held.tile([P, 1], F32, name="warm")
@@ -66,40 +70,44 @@ def tile_picked_sub_mlp_silu_sub_e_kernel(tc, xT, w1, w2, gate, offs, pos1, pos2
         nc.scalar.activation(warm_out[:], warm[:], SILU)
 
         nc.sync.dma_start(offs_sb[:], offs)
-        nc.sync.dma_start(x_plane[0][0][:], x_rows[0, 0])
-        nc.sync.dma_start(w1_raw[0][:], w1_rows[0])
-        for j in range(1, PACK):
-            nc.sync.dma_start(x_plane[0][j][:], x_rows[0, j])
-        nc.sync.dma_start(w1_raw[1][:, 0:2, :], w1_rows[1, :, 0:2, :])
-        for j in range(3):
-            nc.sync.dma_start(x_plane[1][j][:], x_rows[1, j])
-        nc.sync.dma_start(w1_raw[1][:, 2:4, :], w1_rows[1, :, 2:4, :])
-        nc.sync.dma_start(x_plane[1][3][:], x_rows[1, 3])
+        for s, j in ((1, 2), (0, 0), (0, 1), (0, 2), (0, 3)):
+            nc.sync.dma_start(x_plane[s][j][:], x_rows[s, j])
+        for s in (1, 0):
+            nc.sync.dma_start(w1_raw[s][:], w1_rows[s])
+        for s, j in ((1, 0), (1, 1), (1, 3)):
+            nc.sync.dma_start(x_plane[s][j][:], x_rows[s, j])
         nc.sync.dma_start(w2_raw[:], w2.rearrange("(p j) n -> p j n", j=PACK))
         nc.sync.dma_start(pos1_sb[:], pos1)
         nc.sync.dma_start(pos2_sb[:], pos2)
         nc.sync.dma_start(gate_sb[:], gate.rearrange("d n v -> n d v"))
 
-        def pick_plain(s, j):
-            nc.vector.tensor_copy(picked[s][:, j, :], x_plane[s][j][:].indirect(offs_sb[:]))
+        def picked(s, j, a, b):
+            return x_plane[s][j][:].indirect(offs_sb[:, a // 16 : b // 16])
 
-        def pick_stepped(j, c):
-            cols = slice(c * PICK, (c + 1) * PICK)
-            nc.vector.tensor_copy(
-                x_grouped[1][:, cols, j],
-                x_plane[1][j][:].indirect(offs_sb[:, c * PICK // 16 : (c + 1) * PICK // 16]),
-            )
+        def pick_stepped(s, j, a, b):
+            nc.vector.tensor_copy(x_grouped[s][:, a:b, j], picked(s, j, a, b))
 
-        def group_w1(s, a, b):
+        def pick_pair(j):
+            nc.vector.tensor_copy(picked_pair[:, j, :], picked(1, j, 0, 512))
+
+        def pick_all(j):
+            nc.vector.tensor_copy(picked_all[:, j, :], picked(1, j, 512, S))
+
+        def group_w1(s):
             nc.scalar.copy(
-                w1_grouped[s][:, :, :, a:b].rearrange("p t m j -> p m t j"),
-                w1_raw[s][:, a:b, :].rearrange("p j (m t) -> p m t j", t=PACK),
+                w1_grouped[s][:].rearrange("p t m j -> p m t j"),
+                w1_raw[s][:].rearrange("p j (m t) -> p m t j", t=PACK),
             )
 
-        def quantize_w1(s):
+        def quantize_w1(s, t0, t1, tag):
+            codes = held.tile([P, t1 - t0, P], U32, name="w1_codes_%d_%d" % (s, t0), tag=tag, align_bytes=64)
             nc.vector.quantize_mx(
-                out=w1_codes[s][:].bitcast(FP8X4), scales=w1_scales[s][:], in_=w1_grouped[s][:].rearrange("p t m j -> p (t m j)")
+                out=codes[:].rearrange("p t m -> p (t m)").bitcast(FP8X4),
+                scales=w1_scales[s][:, t0:t1, :].rearrange("p t m -> p (t m)"),
+                in_=w1_grouped[s][:, t0:t1, :, :].rearrange("p t m j -> p (t m j)"),
             )
+            for t in range(t0, t1):
+                w1_codes[s, t] = codes[:, t - t0, :]
 
         def quantize_x(s, a, b):
             nc.vector.quantize_mx(
@@ -112,96 +120,109 @@ def tile_picked_sub_mlp_silu_sub_e_kernel(tc, xT, w1, w2, gate, offs, pos1, pos2
             cols = slice(c * CHUNK, (c + 1) * CHUNK)
             nc.tensor.matmul_mx(
                 out=h_bank[c][:, t, :],
-                lhsT=w1_codes[s][:, t * P : (t + 1) * P].bitcast(FP8X4),
-                lhsT_scale=w1_scales[s][:, t * P : (t + 1) * P],
+                lhsT=w1_codes[s, t].bitcast(FP8X4),
+                lhsT_scale=w1_scales[s][:, t, :],
                 rhs=x_codes[s][:, cols].bitcast(FP8X4),
                 rhs_scale=x_scales[s][:, cols],
                 start=(s == 0),
                 stop=(s == 1),
             )
 
-        group_w1(0, 0, 4)
-        pick_plain(0, 0)
-        pick_plain(0, 1)
-        quantize_w1(0)
-        pick_plain(0, 2)
-        pick_plain(0, 3)
-        nc.scalar.copy(
-            x_grouped[0][:].rearrange("p (c i) j -> p c j i", i=4),
-            picked[0][:].rearrange("p j (c i) -> p c j i", i=4),
-        )
-        group_w1(1, 0, 2)
-        pick_plain(1, 0)
-        pick_plain(1, 1)
+        pick_stepped(1, 2, 0, 512)
+        pick_all(2)
+        for j in range(PACK):
+            nc.vector.tensor_copy(x_grouped[0][:, :, j], x_plane[0][j][:].indirect(offs_sb[:]))
         quantize_x(0, 0, 512)
-        quantize_x(0, 512, 768)
-        nc.scalar.copy(x_grouped[1][:, :, 0:2], picked[1][:].rearrange("p j n -> p n j"))
-        for c in range(3):
-            pick_stepped(2, c)
-        group_w1(1, 2, 4)
-        quantize_w1(1)
-        for c in range(CHUNKS):
-            hidden_pass(c, 0, 0)
+        quantize_x(0, 512, S)
+        group_w1(1)
+        quantize_w1(1, 0, 4, "w1_codes_1")
+        group_w1(0)
+        pick_pair(0)
+        pick_all(0)
+        quantize_w1(0, 0, 2, "w1_codes_0")
+        pick_pair(1)
+        pick_all(1)
+        quantize_w1(0, 2, 4, "x_plane_1_1")
+        for a in (0, PICK):
+            nc.scalar.copy(x_grouped[1][:, a : a + PICK, 0:2], picked_pair[:, :, a : a + PICK].rearrange("p j n -> p n j"))
+        for c in range(2):
+            nc.tensor.matmul_mx(
+                out=h_bank[ORDER[4 + c]][:].rearrange("p t n -> p (t n)"),
+                lhsT=w1_codes[0, 3].bitcast(FP8X4),
+                lhsT_scale=w1_scales[0][:, 3, :],
+                rhs=x_codes[0][:, 0:512].bitcast(FP8X4),
+                rhs_scale=x_scales[0][:, 0:512],
+                start=True,
+                stop=True,
+            )
+        for c in ORDER:
+            hidden_pass(c, 3, 0)
 
-        pick_stepped(3, 0)
-        pick_stepped(3, 1)
-        quantize_x(1, 0, 256)
-        pick_stepped(3, 2)
+        pick_stepped(1, 3, 0, 256)
+        pick_all(3)
+        nc.scalar.copy(
+            x_grouped[1][:, 512:S, :].rearrange("p (c i) j -> p c j i", i=4),
+            picked_all[:].rearrange("p j (c i) -> p c j i", i=4),
+        )
+        quantize_x(1, 0, 128)
+        quantize_x(1, 128, 256)
+        pick_stepped(1, 3, 256, 512)
+        quantize_x(1, 512, S)
         quantize_x(1, 256, 512)
-        quantize_x(1, 512, 768)
-        nc.scalar.copy(w2_grouped[:], w2_raw[:].rearrange("p j n -> p n j"))
+        nc.vector.tensor_copy(w2_grouped[:], w2_raw[:].rearrange("p j n -> p n j"))
         nc.vector.quantize_mx(
             out=w2_codes[:].bitcast(FP8X4), scales=w2_scales[:], in_=w2_grouped[:].rearrange("p n j -> p (n j)")
         )
 
-        def hidden(c):
-            hidden_pass(c, 0, 1)
-            for t in range(1, PACK):
+        def hidden(c, cuts):
+            hidden_pass(c, 3, 1)
+            for t in range(3):
                 hidden_pass(c, t, 0)
                 hidden_pass(c, t, 1)
-            nc.scalar.activation(h_grouped[c][:], h_bank[c][:].rearrange("p t n -> p n t"), SILU)
+            for a, b in cuts:
+                nc.scalar.activation(h_grouped[c][:, a:b, :], h_bank[c][:, :, a:b].rearrange("p t n -> p n t"), SILU)
 
-        def quantize_h(c):
-            nc.vector.quantize_mx(
-                out=h_codes[c][:].bitcast(FP8X4), scales=h_scales[c][:], in_=h_grouped[c][:].rearrange("p n t -> p (n t)")
-            )
+        def quantize_h(c, cuts):
+            for a, b in cuts:
+                nc.vector.quantize_mx(
+                    out=h_codes[c][:, a:b].bitcast(FP8X4), scales=h_scales[c][:, a:b], in_=h_grouped[c][:, a:b, :].rearrange("p n t -> p (n t)")
+                )
 
-        def output(c):
-            nc.tensor.matmul_mx(
-                out=y_bank[c % 2][:],
-                lhsT=w2_codes[:].bitcast(FP8X4),
-                lhsT_scale=w2_scales[:],
-                rhs=h_codes[c][:].bitcast(FP8X4),
-                rhs_scale=h_scales[c][:],
-                start=True,
-                stop=True,
-            )
-            nc.vector.tensor_copy(y_sb[:, c * CHUNK : (c + 1) * CHUNK], y_bank[c % 2][:])
+        def output(c, k, cuts):
+            for a, b in cuts:
+                nc.tensor.matmul_mx(
+                    out=y_bank[k % 2][:, a:b],
+                    lhsT=w2_codes[:].bitcast(FP8X4),
+                    lhsT_scale=w2_scales[:],
+                    rhs=h_codes[c][:, a:b].bitcast(FP8X4),
+                    rhs_scale=h_scales[c][:, a:b],
+                    start=True,
+                    stop=True,
+                )
+            nc.vector.tensor_copy(y_sb[:, c * CHUNK : (c + 1) * CHUNK], y_bank[k % 2][:])
 
-        for step in range(CHUNKS + 2):
-            if step < CHUNKS:
-                hidden(step)
-            if 1 <= step <= CHUNKS:
-                quantize_h(step - 1)
+        cuts = [((0, CHUNK),)] * 5 + [((0, 64), (64, CHUNK))]
+        for step in range(8):
+            if step < 6:
+                hidden(ORDER[step], cuts[step])
+            if 1 <= step <= 6:
+                quantize_h(ORDER[step - 1], cuts[step - 1])
             if step >= 2:
-                output(step - 2)
+                output(ORDER[step - 2], step - 2, cuts[step - 2])
 
-        half = V // 2
-        terms = [[held.tile([P, half], F32, name="term_%d_%d" % (a, d)) for d in range(2)] for a in range(2)]
-        sums = [held.tile([P, half], F32, name="sum_%d" % a) for a in range(2)]
+        parts = ((0, 256), (256, V))
+        terms = [[held.tile([P, b - a], F32, name="term_%d_%d" % (a, d)) for d in range(2)] for a, b in parts]
+        sums = [held.tile([P, b - a], F32, name="sum_%d" % a) for a, b in parts]
 
-        def term(a, d):
+        def term(i, d):
+            a, b = parts[i]
             pos = (pos1_sb, pos2_sb)[d]
-            nc.vector.tensor_tensor(
-                terms[a][d][:],
-                y_sb[:].indirect(pos[:, a * half // 16 : (a + 1) * half // 16]),
-                gate_sb[:, d, a * half : (a + 1) * half],
-                MULT,
-            )
+            nc.vector.tensor_tensor(terms[i][d][:], y_sb[:].indirect(pos[:, a // 16 : b // 16]), gate_sb[:, d, a:b], MULT)
 
-        def total(a):
-            nc.vector.tensor_tensor(sums[a][:], terms[a][0][:], terms[a][1][:], ADD)
-            nc.sync.dma_start(out[:, a * half : (a + 1) * half], sums[a][:])
+        def total(i):
+            a, b = parts[i]
+            nc.vector.tensor_tensor(sums[i][:], terms[i][0][:], terms[i][1][:], ADD)
+            nc.sync.dma_start(out[:, a:b], sums[i][:])
 
         term(0, 0)
         term(0, 1)

@@ -50,8 +50,7 @@ def tile_picked_sub_mlp_silu_sub_e_kernel(tc, xT, w1, w2, gate, offs, pos1, pos2
         w2_scales = held.tile([P, N], U8, name="w2_scales", align_bytes=64)
         gate_sb = held.tile([P, 2, V], F32, name="gate_sb")
 
-        picked_pair = held.tile([P, 2, 512], F32, name="picked_pair")
-        picked_all = held.tile([P, PACK, PICK], F32, name="picked_all")
+        picked_sb = held.tile([P, PACK, S], F32, name="picked_sb")
         x_grouped = [held.tile([P, S, PACK], BF16, name="x_grouped_%d" % s, align_bytes=64) for s in range(2)]
         x_codes = [held.tile([P, S], U32, name="x_codes_%d" % s, align_bytes=64) for s in range(2)]
         x_scales = [held.tile([P, S], U8, name="x_scales_%d" % s, align_bytes=64) for s in range(2)]
@@ -87,11 +86,14 @@ def tile_picked_sub_mlp_silu_sub_e_kernel(tc, xT, w1, w2, gate, offs, pos1, pos2
         def pick_stepped(s, j, a, b):
             nc.vector.tensor_copy(x_grouped[s][:, a:b, j], picked(s, j, a, b))
 
-        def pick_pair(j):
-            nc.vector.tensor_copy(picked_pair[:, j, :], picked(1, j, 0, 512))
+        def pick_plain(j, a, b):
+            nc.vector.tensor_copy(picked_sb[:, j, a:b], picked(1, j, a, b))
 
-        def pick_all(j):
-            nc.vector.tensor_copy(picked_all[:, j, :], picked(1, j, 512, S))
+        def group_pair(j, a):
+            nc.scalar.copy(
+                x_grouped[1][:, a : a + PICK, j : j + 2],
+                picked_sb[:, j : j + 2, a : a + PICK].rearrange("p j n -> p n j"),
+            )
 
         def group_w1(s):
             nc.scalar.copy(
@@ -129,7 +131,7 @@ def tile_picked_sub_mlp_silu_sub_e_kernel(tc, xT, w1, w2, gate, offs, pos1, pos2
             )
 
         pick_stepped(1, 2, 0, 512)
-        pick_all(2)
+        pick_plain(2, 512, S)
         for j in range(PACK):
             nc.vector.tensor_copy(x_grouped[0][:, :, j], x_plane[0][j][:].indirect(offs_sb[:]))
         quantize_x(0, 0, 512)
@@ -137,19 +139,17 @@ def tile_picked_sub_mlp_silu_sub_e_kernel(tc, xT, w1, w2, gate, offs, pos1, pos2
         group_w1(1)
         quantize_w1(1, 0, 4, "w1_codes_1")
         group_w1(0)
-        pick_pair(0)
-        pick_all(0)
-        quantize_w1(0, 0, 2, "w1_codes_0")
-        pick_pair(1)
-        pick_all(1)
-        quantize_w1(0, 2, 4, "x_plane_1_1")
-        for a in (0, PICK):
-            nc.scalar.copy(x_grouped[1][:, a : a + PICK, 0:2], picked_pair[:, :, a : a + PICK].rearrange("p j n -> p n j"))
-        for c in range(2):
+        pick_plain(0, 0, S)
+        quantize_w1(0, 0, 4, "x_plane_1_0")
+        pick_plain(1, 0, 256)
+        pick_plain(1, 256, S)
+        for a in (0, PICK, 2 * PICK):
+            group_pair(0, a)
+        for c in range(3):
             nc.tensor.matmul_mx(
-                out=h_bank[ORDER[4 + c]][:].rearrange("p t n -> p (t n)"),
-                lhsT=w1_codes[0, 3].bitcast(FP8X4),
-                lhsT_scale=w1_scales[0][:, 3, :],
+                out=h_bank[ORDER[3 + c]][:].rearrange("p t n -> p (t n)"),
+                lhsT=w1_codes[0, 0].bitcast(FP8X4),
+                lhsT_scale=w1_scales[0][:, 0, :],
                 rhs=x_codes[0][:, 0:512].bitcast(FP8X4),
                 rhs_scale=x_scales[0][:, 0:512],
                 start=True,
@@ -159,11 +159,8 @@ def tile_picked_sub_mlp_silu_sub_e_kernel(tc, xT, w1, w2, gate, offs, pos1, pos2
             hidden_pass(c, 3, 0)
 
         pick_stepped(1, 3, 0, 256)
-        pick_all(3)
-        nc.scalar.copy(
-            x_grouped[1][:, 512:S, :].rearrange("p (c i) j -> p c j i", i=4),
-            picked_all[:].rearrange("p j (c i) -> p c j i", i=4),
-        )
+        pick_plain(3, 512, S)
+        group_pair(2, 2 * PICK)
         quantize_x(1, 0, 128)
         quantize_x(1, 128, 256)
         pick_stepped(1, 3, 256, 512)
@@ -210,23 +207,13 @@ def tile_picked_sub_mlp_silu_sub_e_kernel(tc, xT, w1, w2, gate, offs, pos1, pos2
             if step >= 2:
                 output(ORDER[step - 2], step - 2, cuts[step - 2])
 
+        first = held.tile([P, V], F32, name="first")
+        nc.vector.tensor_tensor(first[:], y_sb[:].indirect(pos1_sb[:]), gate_sb[:, 0, :], MULT)
         parts = ((0, 256), (256, V))
-        terms = [[held.tile([P, b - a], F32, name="term_%d_%d" % (a, d)) for d in range(2)] for a, b in parts]
-        sums = [held.tile([P, b - a], F32, name="sum_%d" % a) for a, b in parts]
-
-        def term(i, d):
-            a, b = parts[i]
-            pos = (pos1_sb, pos2_sb)[d]
-            nc.vector.tensor_tensor(terms[i][d][:], y_sb[:].indirect(pos[:, a // 16 : b // 16]), gate_sb[:, d, a:b], MULT)
-
-        def total(i):
-            a, b = parts[i]
-            nc.vector.tensor_tensor(sums[i][:], terms[i][0][:], terms[i][1][:], ADD)
-            nc.sync.dma_start(out[:, a:b], sums[i][:])
-
-        term(0, 0)
-        term(0, 1)
-        term(1, 0)
-        total(0)
-        term(1, 1)
-        total(1)
+        second = [held.tile([P, b - a], F32, name="second_%d" % a) for a, b in parts]
+        total = [held.tile([P, b - a], F32, name="total_%d" % a) for a, b in parts]
+        for i, (a, b) in enumerate(parts):
+            nc.vector.tensor_tensor(second[i][:], y_sb[:].indirect(pos2_sb[:, a // 16 : b // 16]), gate_sb[:, 1, a:b], MULT)
+        for i, (a, b) in enumerate(parts):
+            nc.vector.tensor_tensor(total[i][:], first[:, a:b], second[i][:], ADD)
+            nc.sync.dma_start(out[:, a:b], total[i][:])

@@ -140,9 +140,10 @@ def tile_picked_sub_mlp_silu_sub_e_kernel(tc, xT, w1, w2, gate, offs, pos1, pos2
         quantize_w1(1, 0, 4, "w1_codes_1")
         group_w1(0)
         pick_plain(0, 0, S)
-        quantize_w1(0, 0, 4, "x_plane_1_0")
+        quantize_w1(0, 0, 2, "x_plane_1_0")
         pick_plain(1, 0, 256)
         pick_plain(1, 256, S)
+        quantize_w1(0, 2, 4, "x_plane_1_1")
         for a in (0, PICK, 2 * PICK):
             group_pair(0, a)
         for c in range(3):

@@ -19,7 +19,7 @@ P = 128
 PACK = 4
 PICK = 256
 CHUNK = 128
-ORDER = (0, 1, 4, 5, 2, 3)
+ORDER = (0, 1, 2, 3, 4, 5)
 
 
 def tile_picked_sub_mlp_silu_sub_e_kernel(tc, xT, w1, w2, gate, offs, pos1, pos2, out):
@@ -61,7 +61,7 @@ def tile_picked_sub_mlp_silu_sub_e_kernel(tc, xT, w1, w2, gate, offs, pos1, pos2
         y_sb = held.tile([P, S], F32, name="y_sb")
 
         h_bank = [psum.tile([P, PACK, CHUNK], F32, name="h_bank_%d" % c) for c in range(6)]
-        y_bank = [psum.tile([P, CHUNK], F32, name="y_bank_%d" % b) for b in range(2)]
+        y_bank = [psum.tile([P, 512], F32, name="y_bank_%d" % b) for b in range(2)]
 
         warm = held.tile([P, 1], F32, name="warm")
         warm_out = held.tile([P, 1], F32, name="warm_out")
@@ -131,7 +131,7 @@ def tile_picked_sub_mlp_silu_sub_e_kernel(tc, xT, w1, w2, gate, offs, pos1, pos2
             )
 
         pick_stepped(1, 2, 0, 512)
-        pick_plain(2, 512, S)
+        pick_stepped(1, 2, 512, S)
         for j in range(PACK):
             nc.vector.tensor_copy(x_grouped[0][:, :, j], x_plane[0][j][:].indirect(offs_sb[:]))
         quantize_x(0, 0, 512)
@@ -141,36 +141,51 @@ def tile_picked_sub_mlp_silu_sub_e_kernel(tc, xT, w1, w2, gate, offs, pos1, pos2
         group_w1(0)
         pick_plain(0, 0, S)
         quantize_w1(0, 0, 2, "x_plane_1_0")
-        pick_plain(1, 0, 256)
-        pick_plain(1, 256, S)
+        pick_plain(1, 0, 512)
+        pick_plain(1, 512, S)
         quantize_w1(0, 2, 4, "x_plane_1_1")
-        for a in (0, PICK, 2 * PICK):
-            group_pair(0, a)
-        for c in range(3):
-            nc.tensor.matmul_mx(
-                out=h_bank[ORDER[3 + c]][:].rearrange("p t n -> p (t n)"),
-                lhsT=w1_codes[0, 0].bitcast(FP8X4),
-                lhsT_scale=w1_scales[0][:, 0, :],
-                rhs=x_codes[0][:, 0:512].bitcast(FP8X4),
-                rhs_scale=x_scales[0][:, 0:512],
-                start=True,
-                stop=True,
-            )
+        group_pair(0, 0)
+        group_pair(0, PICK)
+        group_pair(0, 2 * PICK)
+        nc.tensor.matmul_mx(
+            out=y_bank[0][:],
+            lhsT=w1_codes[0, 0].bitcast(FP8X4),
+            lhsT_scale=w1_scales[0][:, 0, :],
+            rhs=x_codes[0][:, 0:512].bitcast(FP8X4),
+            rhs_scale=x_scales[0][:, 0:512],
+            start=True,
+            stop=True,
+        )
+        nc.tensor.matmul_mx(
+            out=y_bank[1][:],
+            lhsT=w1_codes[0, 0].bitcast(FP8X4),
+            lhsT_scale=w1_scales[0][:, 0, :],
+            rhs=x_codes[0][:, 0:512].bitcast(FP8X4),
+            rhs_scale=x_scales[0][:, 0:512],
+            start=True,
+            stop=True,
+        )
         for c in ORDER:
             hidden_pass(c, 3, 0)
+        nc.tensor.matmul_mx(
+            out=y_bank[0][:],
+            lhsT=w1_codes[0, 3].bitcast(FP8X4),
+            lhsT_scale=w1_scales[0][:, 3, :],
+            rhs=x_codes[0][:, 0:512].bitcast(FP8X4),
+            rhs_scale=x_scales[0][:, 0:512],
+            start=True,
+            stop=True,
+        )
 
         pick_stepped(1, 3, 0, 256)
-        pick_plain(3, 512, S)
-        group_pair(2, 2 * PICK)
         quantize_x(1, 0, 128)
         quantize_x(1, 128, 256)
         pick_stepped(1, 3, 256, 512)
-        quantize_x(1, 512, S)
         quantize_x(1, 256, 512)
-        nc.vector.tensor_copy(w2_grouped[:], w2_raw[:].rearrange("p j n -> p n j"))
-        nc.vector.quantize_mx(
-            out=w2_codes[:].bitcast(FP8X4), scales=w2_scales[:], in_=w2_grouped[:].rearrange("p n j -> p (n j)")
-        )
+        pick_stepped(1, 3, 512, S)
+        quantize_x(1, 512, S)
+        nc.scalar.copy(w2_grouped[:], w2_raw[:].rearrange("p j n -> p n j"))
+        nc.vector.quantize_mx(out=w2_codes[:].bitcast(FP8X4), scales=w2_scales[:], in_=w2_grouped[:].rearrange("p n j -> p (n j)"))
 
         def hidden(c, cuts):
             hidden_pass(c, 3, 1)
@@ -197,16 +212,16 @@ def tile_picked_sub_mlp_silu_sub_e_kernel(tc, xT, w1, w2, gate, offs, pos1, pos2
                     start=True,
                     stop=True,
                 )
-            nc.vector.tensor_copy(y_sb[:, c * CHUNK : (c + 1) * CHUNK], y_bank[k % 2][:])
+            nc.vector.tensor_copy(y_sb[:, c * CHUNK : (c + 1) * CHUNK], y_bank[k % 2][:, 0:CHUNK])
 
         cuts = [((0, CHUNK),)] * 5 + [((0, 64), (64, CHUNK))]
-        for step in range(8):
+        for step in range(9):
             if step < 6:
                 hidden(ORDER[step], cuts[step])
             if 1 <= step <= 6:
                 quantize_h(ORDER[step - 1], cuts[step - 1])
-            if step >= 2:
-                output(ORDER[step - 2], step - 2, cuts[step - 2])
+            if step >= 3:
+                output(ORDER[step - 3], step - 3, cuts[step - 3])
 
         first = held.tile([P, V], F32, name="first")
         nc.vector.tensor_tensor(first[:], y_sb[:].indirect(pos1_sb[:]), gate_sb[:, 0, :], MULT)

from contextlib import ExitStack

import concourse.mybir as mybir

K, T, S, V, H, N = 1024, 2048, 768, 384, 512, 128
FLOPS = 2 * S * H * K + 2 * S * N * H

F32 = mybir.dt.float32
BF16 = mybir.dt.bfloat16
U32 = mybir.dt.uint32
U8 = mybir.dt.uint8
U16 = mybir.dt.uint16
FP8X4 = mybir.dt.float8_e4m3fn_x4
MULT = mybir.AluOpType.mult
ADD = mybir.AluOpType.add
SILU = mybir.ActivationFunctionType.Silu

P = 128
PACK = 4
PICK = 256
CHUNK = 128
ORDER = (0, 1, 2, 3, 4, 5)


def tile_picked_sub_mlp_silu_sub_e_kernel(tc, xT, w1, w2, gate, offs, pos1, pos2, out):
    nc = tc.nc
    with ExitStack() as ctx:
        lists = ctx.enter_context(tc.tile_pool(name="lists", bufs=1))
        held = ctx.enter_context(tc.tile_pool(name="held", bufs=1))
        psum = ctx.enter_context(tc.psum_pool(name="psum", bufs=1))

        offs_sb = lists.tile([P, S // 16], U16, name="offs_sb")
        pos1_sb = lists.tile([P, V // 16], U16, name="pos1_sb")
        pos2_sb = lists.tile([P, V // 16], U16, name="pos2_sb")

        x_rows = xT.rearrange("(s p j) t -> s j p t", s=2, j=PACK)
        w1_rows = w1.rearrange("(s p j) h -> s p j h", s=2, j=PACK)

        x_plane = [
            [held.tile([P, T], F32, name="x_plane_%d_%d" % (s, j), tag="x_plane_%d_%d" % (s, j), align_bytes=64) for j in range(PACK)]
            for s in range(2)
        ]
        w1_raw = [held.tile([P, PACK, H], F32, name="w1_raw_%d" % s) for s in range(2)]
        w1_grouped = [held.tile([P, PACK, P, PACK], BF16, name="w1_grouped_%d" % s, align_bytes=64) for s in range(2)]
        w1_scales = [held.tile([P, PACK, P], U8, name="w1_scales_%d" % s, align_bytes=64) for s in range(2)]
        w1_codes = {}
        w2_raw = held.tile([P, PACK, N], F32, name="w2_raw")
        w2_grouped = held.tile([P, N, PACK], BF16, name="w2_grouped", align_bytes=64)
        w2_codes = held.tile([P, N], U32, name="w2_codes", align_bytes=64)
        w2_scales = held.tile([P, N], U8, name="w2_scales", align_bytes=64)
        gate_sb = held.tile([P, 2, V], F32, name="gate_sb")

        picked_sb = held.tile([P, PACK, S], F32, name="picked_sb")
        x_grouped = [held.tile([P, S, PACK], BF16, name="x_grouped_%d" % s, align_bytes=64) for s in range(2)]
        x_codes = [held.tile([P, S], U32, name="x_codes_%d" % s, align_bytes=64) for s in range(2)]
        x_scales = [held.tile([P, S], U8, name="x_scales_%d" % s, align_bytes=64) for s in range(2)]

        h_grouped = [held.tile([P, CHUNK, PACK], BF16, name="h_grouped_%d" % c, align_bytes=64) for c in range(6)]
        h_codes = [held.tile([P, CHUNK], U32, name="h_codes_%d" % c, align_bytes=64) for c in range(6)]
        h_scales = [held.tile([P, CHUNK], U8, name="h_scales_%d" % c, align_bytes=64) for c in range(6)]
        y_sb = held.tile([P, S], F32, name="y_sb")

        h_bank = [psum.tile([P, PACK, CHUNK], F32, name="h_bank_%d" % c) for c in range(6)]
        y_bank = [psum.tile([P, 512], F32, name="y_bank_%d" % b) for b in range(2)]

        warm = held.tile([P, 1], F32, name="warm")
        warm_out = held.tile([P, 1], F32, name="warm_out")
        nc.vector.memset(warm[:], 0.0)
        nc.scalar.activation(warm_out[:], warm[:], SILU)

        nc.sync.dma_start(offs_sb[:], offs)
        for s, j in ((1, 2), (0, 0), (0, 1), (0, 2), (0, 3)):
            nc.sync.dma_start(x_plane[s][j][:], x_rows[s, j])
        for s in (1, 0):
            nc.sync.dma_start(w1_raw[s][:], w1_rows[s])
        for s, j in ((1, 0), (1, 1), (1, 3)):
            nc.sync.dma_start(x_plane[s][j][:], x_rows[s, j])
        nc.sync.dma_start(w2_raw[:], w2.rearrange("(p j) n -> p j n", j=PACK))
        nc.sync.dma_start(pos1_sb[:], pos1)
        nc.sync.dma_start(pos2_sb[:], pos2)
        nc.sync.dma_start(gate_sb[:], gate.rearrange("d n v -> n d v"))

        def picked(s, j, a, b):
            return x_plane[s][j][:].indirect(offs_sb[:, a // 16 : b // 16])

        def pick_stepped(s, j, a, b):
            nc.vector.tensor_copy(x_grouped[s][:, a:b, j], picked(s, j, a, b))

        def pick_plain(j, a, b):
            nc.vector.tensor_copy(picked_sb[:, j, a:b], picked(1, j, a, b))

        def group_pair(j, a):
            nc.scalar.copy(
                x_grouped[1][:, a : a + PICK, j : j + 2],
                picked_sb[:, j : j + 2, a : a + PICK].rearrange("p j n -> p n j"),
            )

        def group_w1(s):
            nc.scalar.copy(
                w1_grouped[s][:].rearrange("p t m j -> p m t j"),
                w1_raw[s][:].rearrange("p j (m t) -> p m t j", t=PACK),
            )

        def quantize_w1(s, t0, t1, tag):
            codes = held.tile([P, t1 - t0, P], U32, name="w1_codes_%d_%d" % (s, t0), tag=tag, align_bytes=64)
            nc.vector.quantize_mx(
                out=codes[:].rearrange("p t m -> p (t m)").bitcast(FP8X4),
                scales=w1_scales[s][:, t0:t1, :].rearrange("p t m -> p (t m)"),
                in_=w1_grouped[s][:, t0:t1, :, :].rearrange("p t m j -> p (t m j)"),
            )
            for t in range(t0, t1):
                w1_codes[s, t] = codes[:, t - t0, :]

        def quantize_x(s, a, b):
            nc.vector.quantize_mx(
                out=x_codes[s][:, a:b].bitcast(FP8X4),
                scales=x_scales[s][:, a:b],
                in_=x_grouped[s][:, a:b, :].rearrange("p n j -> p (n j)"),
            )

        def hidden_pass(c, t, s):
            cols = slice(c * CHUNK, (c + 1) * CHUNK)
            nc.tensor.matmul_mx(
                out=h_bank[c][:, t, :],
                lhsT=w1_codes[s, t].bitcast(FP8X4),
                lhsT_scale=w1_scales[s][:, t, :],
                rhs=x_codes[s][:, cols].bitcast(FP8X4),
                rhs_scale=x_scales[s][:, cols],
                start=(s == 0),
                stop=(s == 1),
            )

        pick_stepped(1, 2, 0, 512)
        pick_stepped(1, 2, 512, S)
        for j in range(PACK):
            nc.vector.tensor_copy(x_grouped[0][:, :, j], x_plane[0][j][:].indirect(offs_sb[:]))
        quantize_x(0, 0, 512)
        quantize_x(0, 512, S)
        group_w1(1)
        quantize_w1(1, 0, 4, "w1_codes_1")
        group_w1(0)
        pick_plain(0, 0, S)
        quantize_w1(0, 0, 2, "x_plane_1_0")
        pick_plain(1, 0, 512)
        pick_plain(1, 512, S)
        quantize_w1(0, 2, 4, "x_plane_1_1")
        group_pair(0, 0)
        group_pair(0, PICK)
        group_pair(0, 2 * PICK)
        nc.tensor.matmul_mx(
            out=y_bank[0][:],
            lhsT=w1_codes[0, 0].bitcast(FP8X4),
            lhsT_scale=w1_scales[0][:, 0, :],
            rhs=x_codes[0][:, 0:512].bitcast(FP8X4),
            rhs_scale=x_scales[0][:, 0:512],
            start=True,
            stop=True,
        )
        nc.tensor.matmul_mx(
            out=y_bank[1][:],
            lhsT=w1_codes[0, 0].bitcast(FP8X4),
            lhsT_scale=w1_scales[0][:, 0, :],
            rhs=x_codes[0][:, 0:512].bitcast(FP8X4),
            rhs_scale=x_scales[0][:, 0:512],
            start=True,
            stop=True,
        )
        for c in ORDER:
            hidden_pass(c, 3, 0)
        nc.tensor.matmul_mx(
            out=y_bank[0][:],
            lhsT=w1_codes[0, 3].bitcast(FP8X4),
            lhsT_scale=w1_scales[0][:, 3, :],
            rhs=x_codes[0][:, 0:512].bitcast(FP8X4),
            rhs_scale=x_scales[0][:, 0:512],
            start=True,
            stop=True,
        )

        pick_stepped(1, 3, 0, 256)
        quantize_x(1, 0, 128)
        quantize_x(1, 128, 256)
        pick_stepped(1, 3, 256, 512)
        quantize_x(1, 256, 512)
        pick_stepped(1, 3, 512, S)
        quantize_x(1, 512, S)
        nc.scalar.copy(w2_grouped[:], w2_raw[:].rearrange("p j n -> p n j"))
        nc.vector.quantize_mx(out=w2_codes[:].bitcast(FP8X4), scales=w2_scales[:], in_=w2_grouped[:].rearrange("p n j -> p (n j)"))

        def hidden(c, cuts):
            hidden_pass(c, 3, 1)
            for t in range(3):
                hidden_pass(c, t, 0)
                hidden_pass(c, t, 1)
            for a, b in cuts:
                nc.scalar.activation(h_grouped[c][:, a:b, :], h_bank[c][:, :, a:b].rearrange("p t n -> p n t"), SILU)

        def quantize_h(c, cuts):
            for a, b in cuts:
                nc.vector.quantize_mx(
                    out=h_codes[c][:, a:b].bitcast(FP8X4), scales=h_scales[c][:, a:b], in_=h_grouped[c][:, a:b, :].rearrange("p n t -> p (n t)")
                )

        def output(c, k, cuts):
            for a, b in cuts:
                nc.tensor.matmul_mx(
                    out=y_bank[k % 2][:, a:b],
                    lhsT=w2_codes[:].bitcast(FP8X4),
                    lhsT_scale=w2_scales[:],
                    rhs=h_codes[c][:, a:b].bitcast(FP8X4),
                    rhs_scale=h_scales[c][:, a:b],
                    start=True,
                    stop=True,
                )
            nc.vector.tensor_copy(y_sb[:, c * CHUNK : (c + 1) * CHUNK], y_bank[k % 2][:, 0:CHUNK])

        cuts = [((0, CHUNK),)] * 5 + [((0, 64), (64, CHUNK))]
        for step in range(9):
            if step < 6:
                hidden(ORDER[step], cuts[step])
            if 1 <= step <= 6:
                quantize_h(ORDER[step - 1], cuts[step - 1])
            if step >= 3:
                output(ORDER[step - 3], step - 3, cuts[step - 3])

        first = held.tile([P, V], F32, name="first")
        nc.vector.tensor_tensor(first[:], y_sb[:].indirect(pos1_sb[:]), gate_sb[:, 0, :], MULT)
        parts = ((0, 256), (256, V))
        second = [held.tile([P, b - a], F32, name="second_%d" % a) for a, b in parts]
        total = [held.tile([P, b - a], F32, name="total_%d" % a) for a, b in parts]
        for i, (a, b) in enumerate(parts):
            nc.vector.tensor_tensor(second[i][:], y_sb[:].indirect(pos2_sb[:, a // 16 : b // 16]), gate_sb[:, 1, a:b], MULT)
        for i, (a, b) in enumerate(parts):
            nc.vector.tensor_tensor(total[i][:], first[:, a:b], second[i][:], ADD)
            nc.sync.dma_start(out[:, a:b], total[i][:])
